import numpy as np, ml_dtypes
CORES = [24,25,26,27,28,29,30,31]
N = 8
BF = ml_dtypes.bfloat16
C, P, WA, WM, MC, RO = 128, 16, 4096, 4096, 16, 3
L0, LM, AM, Q, B = 3, 7, 3, 4096 // 128, 16 // 16
def block(rng, n):
    q = rng.integers(24, 257, (N, 8, 16, n // P, 1))
    return (rng.random((N, 8, 16, n // P, P)) * q).astype(np.int64).reshape(N, 8, 16, n)
def parts(rng):
    X = block(rng, C * P); A = block(rng, WA); M = rng.integers(0, 256, (N, 8, 16, WM))
    w = rng.integers(0, 256, (N, 8, 16, 2)); k = rng.integers(0, 2048, (N, 8, 2, MC))
    t = np.stack([rng.integers(700, 1101, (N, 8)), rng.integers(700, 1001, (N, 8))], axis=2)
    return X, A, M, w, k, t
def pack(X, A, M, w, k, t):
    b = lambda v: np.ascontiguousarray(v.reshape(N, 128, -1)).astype(np.float32).astype(BF)
    h = k.reshape(N, 8, 2, B, 16).transpose(0, 1, 4, 2, 3).reshape(N, 128, 2 * B)
    return {"gn": b(X), "ar": b(A), "mh": b(M), "wt": b(w), "hk": np.ascontiguousarray(h).astype(np.int32), "th": np.repeat(t, 16, axis=1).astype(np.int32)}
def setup_inputs(rng):
    return pack(*parts(rng))
def setup_inputs_ties(rng):
    X, A, M, w, k, t = parts(rng)
    return pack((X >> 4) << 4, (A >> 4) << 4, (M >> 4) << 4, w | 1, k, (t >> 4) << 4)
def setup_inputs_ends(rng):
    X, A, M, w, k, t = parts(rng); E = X.reshape(N, 8, 16, C, P); c = np.arange(C); uu = np.arange(4096)
    k[:, 1::2, :, 0] = 0; k[:, 1::2, :, MC - 1] = 2047
    for q in range(N):
        for g in range(0, 8, 2):
            o = (2 * rng.permutation(2048)[:64] + 1) | (LM << 4)
            s = ((o * o >> 5)[:, None] + o[:, None] * np.arange(2048)[None, :]) & (WA - 1)
            j = int(np.argmax(s)); key = j % 2048; k[q, g, 0] = key
            near = np.argsort(((uu * uu >> 5) + key * uu) & (WA - 1))[-64:]
            u = near[rng.integers(0, 64, C)]; u[0] = 0; u[1] = o[j // 2048]; u[C - 1] = o[j // 2048]
            w[q, g, :, 0] = 0; w[q, g, 0, 0] = 1; w[q, g, 1, 0] = 128
            E[q, g, 0, c, c & AM] = u & 127; E[q, g, 1, c, c & AM] = u >> 7
    t[:, ::2, 0] = 4096; t[:, 0, 1] = 0
    return pack(E.reshape(N, 8, 16, C * P), A, M, w, k, t)
def setup_inputs_edges(rng):
    X, A, M, w, k, t = parts(rng)
    t[:, 0, 0] = 0; t[:, 1, 1] = 4096; t[:, 2, 0] = 4096; t[:, 2, 1] = 0; t[:, 3] = 1
    pat = rng.integers(0, 256, (16, 2)); pat[0, 0] = 3; pat[0, 1] = 200
    X[:, 3] = np.where(rng.random((N, 1, C * P)) < 0.5, pat[None, :, :1], pat[None, :, 1:])
    A[:, 3] = np.where(rng.random((N, 1, WA)) < 0.5, pat[None, :, :1], pat[None, :, 1:])
    M[:, 3] = np.where(rng.random((N, 1, WM)) < 0.06, np.max(pat, axis=1)[None, :, None], M[:, 3])
    w[:, 4] = rng.integers(240, 256, (N, 16, 2))
    X[:, 4] = rng.integers(200, 256, (N, 16, C * P)); A[:, 4] = rng.integers(200, 256, (N, 16, WA)); M[:, 4] = rng.integers(200, 256, (N, 16, WM))
    t[:, 4, 0] = rng.integers(230, 331, N); t[:, 4, 1] = rng.integers(230, 301, N)
    for g, lo in ((5, 150), (7, 70)):
        lev = int(rng.integers(lo, 241))
        X[:, g] = rng.integers(0, 16, (N, 16, C * P)) + (lev if g == 7 else 0)
        A[:, g] = rng.integers(0, 16, (N, 16, WA)) + (lev if g == 5 else 0)
        M[:, g] = rng.integers(0, 16, (N, 16, WM))
        t[:, g, 0] = 16 * lev + 4 * rng.integers(-5, 6, N) + rng.integers(0, 2, N)
        t[:, g, 1] = 16 * lev + 4 * rng.integers(10, 19, N) + rng.integers(0, 2, N)
    pa = rng.integers(0, 256, (16, 8))
    jx = np.repeat(rng.integers(0, 8, (N, C)), P, axis=1); ja = np.repeat(rng.integers(0, 8, (N, WA // P)), P, axis=1)
    jx = np.where((np.arange(C * P) // P) % 8 < 4, jx, rng.integers(0, 8, (N, C * P)))
    X[:, 6] = pa[:, jx].transpose(1, 0, 2); A[:, 6] = pa[:, ja].transpose(1, 0, 2)
    t[:, 6, 0] = 1; t[:, 6, 1] = 0
    return pack(X, A, M, w, k, t)
def setup_inputs_alike(rng):
    X, A, M, w, k, t = parts(rng); E = X.reshape(N, 8, 16, C, P); H = A.reshape(N, 8, 16, WA // P, P)
    E[:, ::2] = np.repeat(E[:, ::2, :, :1], C, axis=3); E[:, :, :, 5::8] = 0
    H[:, 1::2] = np.tile(H[:, 1::2, :, :4], (1, 1, 1, WA // P // 4, 1))
    M[:, 3::4] = M[:, 3::4][..., rng.integers(0, 8, WM)]
    k[..., 1::2] = k[..., ::2]
    return pack(E.reshape(N, 8, 16, C * P), H.reshape(N, 8, 16, WA), M, w, k, t)
def setup_inputs_spread(rng):
    X, A, M, w, k, t = parts(rng)
    X = (np.exp2(8 * rng.random((N, 8, 1, C * P))) * rng.random(X.shape)).astype(np.int64)
    A = (np.exp2(8 * rng.random((N, 8, 1, WA))) * rng.random(A.shape)).astype(np.int64)
    M = (np.exp2(4 + 4 * rng.random((N, 8, 1, WM))) * (0.5 + 0.5 * rng.random(M.shape))).astype(np.int64)
    w = np.exp2(8 * rng.random(w.shape)).astype(np.int64); k = np.exp2(11 * rng.random(k.shape)).astype(np.int64)
    t = np.stack([np.exp2(6.5 + 3.5 * rng.random((N, 8))), np.exp2(9 + 2 * rng.random((N, 8)))], axis=2).astype(np.int64)
    return pack(np.minimum(X, 255), np.minimum(A, 255), np.minimum(M, 255), np.minimum(w, 255), np.minimum(k, 2047), t)
def check_inputs(d):
    bad = []
    for s in ("gn", "ar", "mh", "wt"):
        v = d[s].astype(np.float32)
        if not (np.all(v >= 0) and np.all(v <= 255) and np.all(v == np.floor(v))): bad.append("whole numbers from 0 to 255 in " + s)
    for s, hi in (("hk", 2047), ("th", 4096)):
        if np.min(d[s]) < 0 or np.max(d[s]) > hi: bad.append("range of " + s)
    v = d["th"].reshape(N, 8, 16, 2)
    if not np.all(v == v[:, :, :1]): bad.append("th alike in the rows of a group")
    return bad
def pick(a, ix):
    return np.take_along_axis(a, ix.reshape(N, 8, 1, -1), 3).reshape((N, 8, 16) + ix.shape[2:])
def reference(gn, ar, mh, wt, hk, th):
    ints = lambda v: v.astype(np.float32).astype(np.int64)
    X = ints(gn).reshape(N, 8, 16, C, P); A = ints(ar).reshape(N, 8, 16, WA); M = ints(mh).reshape(N, 8, 16, WM); w = ints(wt).reshape(N, 8, 16, 2)
    k = hk.astype(np.int64).reshape(N, 8, 16, 2, B).transpose(0, 1, 3, 4, 2).reshape(N, 8, 2, MC)
    lim = th.astype(np.int64).reshape(N, 8, 16, 2)[:, :, 0, :, None, None]
    c = np.arange(C); m = np.arange(MC); i = np.arange(P)
    for t in range(RO):
        d = 1 + t % (N - 1); a = (c + 3 * t) & AM
        xa = X[:, :, :, c, a]
        u = np.add.reduce(w[..., 0:1] * xa, axis=2) & 4095
        p = ((u * u >> 5)[..., None] + k[:, :, 0, None, :] * u[..., None]) & (WA - 1)
        l = L0 + ((u[..., None] * (2 * m + 1) >> 4) & LM)
        d1 = np.add.reduce(np.abs(pick(A, p) - xa[..., None]), axis=2)
        xe = pick(X.reshape(N, 8, 16, C * P), (P * c + a)[:, None] + l)
        d2 = np.add.reduce(np.abs(pick(A, (p + l) & (WA - 1)) - xe), axis=2)
        score = np.where((d1 < lim[:, :, 0]) & (d2 < lim[:, :, 0]), l * MC + (MC - 1 - m), -1)
        best = np.argmax(score, axis=3)[..., None]
        lb = np.where(np.max(score, axis=3)[..., None] >= 0, np.take_along_axis(l, best, 3), 0); pb = np.take_along_axis(p, best, 3)
        inside = (i > a[:, None]) & (i < a[:, None] + lb)
        trial = np.where(inside[:, :, None], pick(A, (pb + i - a[:, None]) & (WA - 1)), X)
        z = np.roll(np.max(trial, axis=4), d, axis=0)
        v = np.add.reduce(w[..., 1:2] * z, axis=2) & 4095
        pm = ((v * v >> 5)[..., None] + k[:, :, 1, None, :] * v[..., None]) & (WM - 1)
        dm = np.add.reduce(np.abs(pick(M, pm) - z[..., None]), axis=2)
        known = np.any(dm < lim[:, :, 1], axis=3)
        np.put_along_axis(M, (C * (v & (Q - 1)) + c)[:, :, None, :], z, 3)
        new = np.roll(np.logical_not(known), -d, axis=0)
        X = np.where(new[:, :, None, :, None], trial, X)
        over = new & ((c & 3) == (t & 3))
        head = np.where(over[:, :, None, :, None], trial, A[..., :C * P].reshape(N, 8, 16, C, P))
        A = np.concatenate([head.reshape(N, 8, 16, C * P), A[..., C * P:]], axis=3)
    return {"y": np.ascontiguousarray(X).reshape(N, 128, C * P).astype(np.float32).astype(BF)}

import math
from concourse.bass import DstId, RemoteDMATransfer
from concourse.mybir import AluOpType, ActivationFunctionType

N = 8
XB, AB, WEND = 6144, 8192, 12304
BIG = float(2 ** 22)
HUGE = float(2 ** 56)
LN2 = math.log(2.0)

CFG = {"chunk": 512, "yg": 256, "ys": (0, 512, 2048), "nd": 2,
       "banks": ["S0 L0 S20 D10 P0 lf0 o10 o20", "D20 V0 DM0 X0 X20", "S1 L1 S21 D11 P1 lf1 o11 o21",
                 "D21 V1 DM1 dg1 X1 X21", "ku0 kv0 Q0 E0", "ku1 kv1 Q1 E1"]}
ORDER = """
28 48 42 7 0 1 2 3 4 5 6 34 11 35 30 12 44 13 36 15 46 8 9 29 26 37 14 38 39 40 49 27 43 50 10 65 63 81 71 31 24 32 33 45
75 66 87 25 94 47 74 68 86 64 67 83 82 23 95 77 76 78 16 96 72 88 84 100 102 132 79 114 80 97 69 85 139 133 140 90 20 135
134 89 101 111 141 136 137 138 143 145 21 146 156 142 91 92 93 104 103 18 17 147 98 22 51 144 148 99 112 115 149 105 106
107 108 150 53 116 113 152 153 109 151 159 19 160 161 157 158 54 41 73 56 117 118 52 60 110 119 120 154 155 162 164 121
122 163 165 166 123 125 124 167 168 126 169 127 170 171 172 173 130 131 174 128 129 177 179 180 175 176 181 227 183 182
184 185 186 55 188 178 58 187 191 192 229 230 228 231 232 233 234 261 189 190 257 258 259 235 236 237 260 70 262 193 194
195 197 207 208 204 199 238 239 209 217 241 196 268 275 269 198 270 276 200 277 219 271 240 215 201 220 224 221 214 223
211 272 202 281 273 222 216 242 218 283 274 225 210 212 213 278 295 279 280 243 244 245 247 249 282 226 296 252 285 284
286 248 246 288 250 313 314 320 315 316 321 254 292 293 317 322 318 297 287 289 290 326 319 251 294 298 330 327 329 331
291 328 300 57 59 203 337 324 299 61 301 302 303 340 333 323 332 305 304 263 266 306 307 325 334 335 308 309 341 338 311
310 342 339 312 358 336 345 360 205 361 253 362 364 363 365 366 367 369 368 343 344 346 255 347 348 349 350 62 264 265
351 352 353 354 356 355 372 206 373 370 371 357 267 403 359 431 402 404 256 405 406 408 407 409 410 411 413 412 374 375
376 378 427 428 377 379 435 380 381 436 442 383 438 384 437 385 390 386 443 439 444 382 440 448 416 389 417 394 399 441
449 446 459 450 387 447 414 429 400 388 415 396 445 398 401 395 462 393 391 397 392 451 460 418 419 422 424 420 452 453
463 461 421 423 480 464 454 425 426 455 456 483 487 481 488 482 489 430 484 493 485 465 494 486 491 495 457 497 496 498
466 458 507 504 467 492 468 469 470 499 505 500 490 501 506 471 473 472 502 508 509 474 475 478 476 503 432 433 512 434
510 511 513 514 477 515 516 518 517 479 525 519 520 526 527 528 530 529 531 532 533 521 522 534 523 524 544 545 535 536
537 546 547 549 538 548 550 551 552 553 554 555 539 557 556 540 558 559 560 541 542 543 564 561 562 565 566 563 568 567
575 573 569 571 574 570 572 576
"""
QUEUES = ("SAASSSSVGGVGVVVVVVGVVVVGGVVVVVVGGVGVVVVVAGVVVVVVGGVGNGGNGNGNVVVPPPVAAAGAVGGPPPVAAAGAGGGVVVVVVVVVVAVVVVVAAPAPAPVA"
          "VAAVAPVVVPAVVPVVAVAVVVVVVVVVVVAVVVVVVAPAPAPAAVAVVAPVVVPVVVPVVVVAVPAVVVVVVVVVAPAPAPVPVPVPVAPVPVAVVAGVGGVAVGVVAVV"
          "VAGGPVVVVVVVVVVAPAPAPVPVPVPVAPVPVAVVPVGGNGNVVVVVVVVVVVVAVVVVVAAPAPAPVAVAVVAPVVVPAVVPVVAVAVVVVVVVVVVVAVVVVVVAPAP"
          "APVAVAVVAPVVVPVVVPVVVVAVPAVVVVVVVVAAPAPAPVPVPVPVAVVAGVAAGGGGAVAGVAAVPAVVVVVVVVAAPAPAPVPVPVPVAVVPVGGNVVVVVVVVVVV"
          "AVVVVVAAPAPAPAVVAVVAPAVVPAVVPVVAVVVVVVVVVVVVVAVVVVVVAPAPAPVVVAAVAPAVVPVVVPVVAVAVPVVVVVVVVVAPAPAPVPVPVVVVVVVVAVP"
          "APAPAPVVVVVVAAAAVVVSS")

SCRATCH = {
    "W": ("sbuf", [128, WEND], "bfloat16"),
    "mown": ("sbuf", [128, 4096], "bfloat16"),
    "wts": ("sbuf", [128, 2], "bfloat16"),
    "hks": ("sbuf", [128, 2], "int32"),
    "ths": ("sbuf", [128, 2], "int32"),
    "par": ("sbuf", [128, 3], "float32"),
    "cols": ("sbuf", [128, 8], "float32"),
    "pcol": ("sbuf", [128, 2], "int32"),
    "BOf": ("sbuf", [128, 128], "float32"),
    "Z": ("sbuf", [128, 144], "bfloat16"),
    "Wj": ("sbuf", [128, 384], "bfloat16"),
    "at": ("sbuf", [128, 160], "bfloat16"),
    "TH": ("sbuf", [128, 160], "bfloat16"),
    "dl": ("sbuf", [128, 480], "float32"),
    "cst": ("sbuf", [128, 256], "bfloat16"),
    "msk": ("sbuf", [128, 512], "bfloat16"),
    "st": ("sbuf", [128, 512], "float32"),
    "acon": ("sbuf", [128, 64], "float32"),
    "cdf": ("sbuf", [128, 8], "float32"),
    "cd": ("sbuf", [128, 8], "bfloat16"),
    "sold": ("sbuf", [128, 384], "float32"),
    "xa": ("sbuf", [128, 384], "bfloat16"),
    "xo": ("sbuf", [128, 384], "bfloat16"),
    "xy": ("sbuf", [128, 256], "bfloat16"),
    "ia": ("sbuf", [128, 1280], "int32"),
    "ib": ("sbuf", [128, 1280], "int32"),
    "vi": ("sbuf", [128, 384], "int32"),
    "v32": ("sbuf", [128, 128], "int32"),
    "fa": ("sbuf", [128, 1024], "float32"),
    "ba": ("sbuf", [128, 256], "bfloat16"),
    "L": ("sbuf", [128, 1024], "uint16"),
    "Ly": ("sbuf", [128, 128], "uint16"),
    "atmp": ("sbuf", [128, 512], "bfloat16"),
}
for _b in ("ones", "tmpa", "tmpb", "tmpc", "tmpd", "BO", "BOB", "ID", "NI", "BP", "Wb", "s16", "v32b"):
    SCRATCH[_b] = ("sbuf", [128, 128], "bfloat16")
for _b in ("xe", "d1", "d2", "r1", "r2", "sc", "mg", "dm", "yb"):
    SCRATCH[_b] = ("sbuf", [128, 2048], "bfloat16")
for _k in range(3):
    SCRATCH["mc%d" % _k] = ("sbuf", [128, 4096], "bfloat16")
    SCRATCH["pj%d" % _k] = ("sbuf", [128, 3], "float32")
    SCRATCH["zl%d" % _k] = ("sbuf", [128, 128], "bfloat16")
    SCRATCH["ml%d" % _k] = ("sbuf", [128, 8], "uint16")
for _k in range(2):
    SCRATCH["zc%d" % _k] = ("sbuf", [128, 128], "bfloat16")
    SCRATCH["mo%d" % _k] = ("sbuf", [128, 8], "uint16")
for _k in range(8):
    SCRATCH["ps%d" % _k] = ("psum", [128, 512], "float32")

SEMAPHORES = ["cV", "cA", "cP", "cG", "sent", "ap", "aq", "am0", "am1", "am2", "az0", "az1",
              "lgn", "lar", "lwt", "lhk", "lth", "lm0", "lm1"] + ["sy%d" % _k for _k in range(len(CFG["ys"]) - 1)]

BYTES = {"bfloat16": 2, "uint16": 2, "float32": 4, "int32": 4}


def S(buf, lo, hi, step=1):
    return ("s", buf, lo, hi, step)


def IND(buf, lo, hi, ob, olo, ohi):
    return ("i", buf, lo, hi, ob, olo, ohi)


def bits(lo, hi, step):
    if step == 1:
        return ((1 << (hi - lo)) - 1) << lo
    m = 0
    for x in range(lo, hi, step):
        m |= 1 << x
    return m


def count(o):
    if o[0] == "i":
        return 16 * (o[6] - o[5])
    return len(range(o[2], o[3], o[4]))


def regions(o):
    if not isinstance(o, tuple):
        return []
    if o[0] == "i":
        return [(o[1], bits(o[2], o[3], 1)), (o[4], bits(o[5], o[6], 1))]
    return [(o[1], bits(o[2], o[3], o[4]))]


def build_ops(cfg):
    ops = []
    A = AluOpType
    tag = ["init"]

    def add(k, engs, a, w, r, **kw):
        wr = []; rd = []
        for o in w:
            g = regions(o); wr.append(g[0]); rd += g[1:]
        for o in r:
            rd += regions(o)
        d = {"k": k, "engs": engs, "a": a, "w": wr, "r": rd, "after": [], "n": len(ops), "tag": tag[0]}
        d.update(kw)
        ops.append(d)
        return d

    def tt(o, x, y, op): return add("tt", "V", (o, x, y, op), [o], [x, y])
    def ts(o, x, s1, s2, op0, op1=None): return add("ts", "V", (o, x, s1, s2, op0, op1), [o], [x, s1, s2])
    def cp(o, x, engs="V"): return add("cp", engs, (o, x), [o], [x])
    def ms(o, v): return add("ms", "V", (o, v), [o], [])
    def act(o, x, f, bias=0.0, scale=1.0): return add("act", "A", (o, x, f, bias, scale), [o], [x, bias, scale])
    def mm(lst): return add("mm", "P", lst, [m[0] for m in lst], [m[1] for m in lst] + [m[2] for m in lst])
    def iota(o, pat, base, cm): return add("iota", "G", (o, pat, base, cm), [o], [])
    def sel(o, x, pat, op, fill, base, cm): return add("sel", "G", (o, x, pat, op, fill, base, cm), [o], [x])
    def group(out, terms):
        return mm([(o if o is not None else out, l, r, j == 0, j == len(terms) - 1) for j, (o, l, r) in enumerate(terms)])

    def test(o, x, s1, big, op0, bias, scale):
        return add("ts", "VA", (o, x, s1, big, op0, A.mult), [o], [x, s1, bias], alt=(o, x, "Relu", bias, scale))

    def load(q, sem, o, name, lo, hi):
        return add("dma", q, (o, name, lo, hi, True), [o], [], sem=sem, nb=128 * (hi - lo) * BYTES[SCRATCH[o[1]][2]])

    def send(src, dsts, sem):
        nb = 128 * count(src) * BYTES[SCRATCH[src[1]][2]] * len(dsts)
        return add("rem", "G", (src, dsts, sem), [], [src], nb=nb)

    def arrive(sem, srcs, bufs, sends):
        d = add("arr", "N", (srcs,), bufs, [], sem=sem)
        d["after"] = [s["n"] for s in sends]
        return d

    full = lambda b: S(b, 0, SCRATCH[b][1][1])
    M128 = lambda b: S(b, 0, 128)
    load("S", "lgn", S("W", XB, AB), "gn", 0, 2048)
    load("A", "lwt", full("wts"), "wt", 0, 2)
    load("A", "lhk", full("hks"), "hk", 0, 2)
    load("S", "lar", S("W", AB, AB + 4096), "ar", 0, 4096)
    load("S", "lth", full("ths"), "th", 0, 2)
    load("S", "lm0", S("mown", 0, 2048), "mh", 0, 2048)
    load("S", "lm1", S("mown", 2048, 4096), "mh", 2048, 4096)
    icol, mcol, c4r, kcol, tcol, btcol = [S("cols", j, j + 1) for j in range(6)]
    ms(M128("ones"), 1.0)
    sel(M128("tmpa"), M128("ones"), [[-16, 8], [0, 16]], A.is_ge, 0.0, 0, 1)
    sel(M128("BO"), M128("tmpa"), [[16, 8], [0, 16]], A.is_ge, 0.0, 15, -1)
    ts(M128("Wb"), M128("BO"), S("wts", 0, 1), None, A.mult)
    iota(S("pcol", 0, 1), [[1, 1]], 0, 1)
    ts(S("pcol", 1, 2), S("pcol", 0, 1), 15, None, A.bitwise_and)
    cp(icol, S("pcol", 1, 2))
    ts(mcol, icol, 2.0, 1.0, A.mult, A.add)
    ts(c4r, icol, 4.0, None, A.mult)
    cp(kcol, S("hks", 0, 1)); cp(tcol, S("ths", 0, 1))
    cp(S("W", AB + 4096, WEND), S("W", AB, AB + 16), "GAV")
    ts(btcol, S("ths", 0, 1), HUGE, None, A.mult)
    cp(S("par", 0, 1), S("wts", 1, 2)); cp(S("par", 1, 2), S("hks", 1, 2)); cp(S("par", 2, 3), S("ths", 1, 2))
    iota(S("st", 0, 128), [[16, 4], [64, 32]], -2048, 0)
    sel(M128("ID"), M128("ones"), [[-1, 128]], A.is_equal, 0.0, 0, 1)
    ts(M128("NI"), M128("ID"), -1.0, None, A.mult)
    ts(M128("BOB"), M128("BO"), BIG, None, A.mult)
    cp(M128("BOf"), M128("BO"))
    ms(full("Z"), 0.0)
    cp(S("Z", 15, 143, 16), S("BO", 0, 128, 16))
    ms(M128("tmpb"), 1.0 / 32)
    sel(M128("tmpc"), M128("tmpb"), [[-1, 128]], A.is_gt, 1.0, 0, 1)
    sel(M128("tmpd"), M128("tmpc"), [[-1, 128]], A.not_equal, -0.75, 0, 1)
    tt(M128("BP"), M128("tmpd"), M128("BO"), A.mult)
    iota(S("at", 0, 128), [[1, 4], [0, 32]], 0, 0)
    ms(S("at", 128, 160), 0.0)
    ts(S("dl", 0, 160), full("at"), -1.0, icol, A.mult, A.add)
    ts(S("dl", 160, 320), S("dl", 0, 160), -2.0, 0.0, A.add, A.max)
    ts(S("dl", 320, 480), S("dl", 0, 160), 0.0, 11.0, A.is_le, A.mult)
    tt(S("dl", 0, 160), S("dl", 160, 320), S("dl", 320, 480), A.add)
    act(full("TH"), S("dl", 0, 160), "Exp", math.log(0.75) + 17 * LN2, 5 * LN2)
    iota(M128("s16"), [[16, 128]], 0, 0)
    for t in range(3):
        ms(S("cst", 64 * t, 64 * t + 64), 2048.0 * (t + 2))
    ms(S("cst", 192, 256), 65536.0)
    ms(full("msk"), 1.0)
    ms(S("msk", 0, 512, 16), 0.0)
    iota(full("acon"), [[16, 2], [64, 32]], 0, 0)
    iota(full("cdf"), [[1, 4], [64, 2]], 0, 0)
    ts(full("cd"), full("cdf"), 0.125, None, A.mult)
    s = send(full("par"), [(1, full("pj0"))], "ap")
    arrive("ap", [1], [full("pj0")], [s])
    sa = send(S("mown", 0, 2048), [(1, S("mc0", 0, 2048))], "am0")
    sb = send(S("mown", 2048, 4096), [(1, S("mc0", 2048, 4096))], "am0")
    arrive("am0", [1, 1], [full("mc0")], [sa, sb])
    s1 = send(full("mown"), [(2, full("mc1"))], "am1"); s1["after"] = [sb["n"]]
    arrive("am1", [2], [full("mc1")], [s1])
    s = send(full("par"), [(2, full("pj1")), (3, full("pj2"))], "aq"); s["after"] = [sb["n"]]
    arrive("aq", [2, 3], [full("pj1"), full("pj2")], [s])
    for k in range(3):
        ts(S("Wj", 128 * k, 128 * k + 128), M128("BO"), S("pj%d" % k, 0, 1), None, A.mult)

    aof = lambda cls, t: (cls + 3 * t) % 4
    sel_m = lambda m: S("Z", 15 - m, 143 - m)
    place = {}
    for b, names in enumerate(cfg["banks"]):
        for j, name in enumerate(names.split()):
            place[name] = (cfg["nd"] + b, j)

    def ps(h, name, lo=0, hi=64):
        b, j = place[name + str(h)]
        return S("ps%d" % b, 64 * j + lo, 64 * j + hi)

    def xcols(cls, a): return S("W", XB + 16 * cls + a, AB, 64)
    def tcols(t, cls, a): return S("W", (2 - t) * 2048 + 512 * cls + a, (2 - t) * 2048 + 512 * cls + 512, 16)
    def ia(h, j): return S("ia", 640 * h + 64 * j, 640 * h + 64 * j + 64)
    def ib(h, j): return S("ib", 640 * h + 64 * j, 640 * h + 64 * j + 64)
    def fa(h, j, lo=0, hi=64): return S("fa", 512 * h + 64 * j + lo, 512 * h + 64 * j + hi)
    def LL(h, j, lo=0, hi=64): return S("L", 512 * h + 64 * j + lo, 512 * h + 64 * j + hi)
    def half(b, t, h, lo=0, hi=64): return S(b, 128 * t + 64 * h + lo, 128 * t + 64 * h + hi)
    ch = cfg["chunk"]
    chunks = [(x, x + ch) for x in range(0, 1024, ch)]
    turn = [0]

    def gl(h, j, lo, hi): return ("L", 512 * h + 64 * j + lo // 16, 512 * h + 64 * j + hi // 16)

    def hash_list(h, src, u, key, scratch, pk, out16):
        ts(u, src, 4095, None, A.bitwise_and)
        tt(scratch(h, 2), u, u, A.mult)
        ts(scratch(h, 3), scratch(h, 2), 5, None, A.arith_shift_right)
        ts(ps(h, pk), u, key, None, A.mult)
        tt(scratch(h, 4), scratch(h, 3), ps(h, pk), A.add)
        ts(scratch(h, 5), scratch(h, 4), 4095, None, A.bitwise_and)
        cp(out16, scratch(h, 5))

    def distance(h, gathered, col, absb, D):
        o = 1024 * h
        for b in range(2):
            bank = "ps%d" % (turn[0] % cfg["nd"]); turn[0] += 1
            lst = []
            for m in range(8 * b, 8 * b + 8):
                out = S(bank, 64 * (m % 8), 64 * (m % 8) + 64)
                lst += [(out, M128("NI"), col, True, False), (out, M128("ID"), S(gathered, o + m, o + 1024, 16), False, True)]
            mm(lst)
            act(S(absb, o + 512 * b, o + 512 * b + 512), S(bank, 0, 512), "Abs")
        group(ps(h, D), [(None, sel_m(m), S(absb, o + 64 * m, o + 64 * m + 64)) for m in range(16)])

    for h in range(2):
        for name, t in (("S", 0), ("o1", 1), ("o2", 2)):
            mm([(ps(h, name, 32 * j, 32 * j + 32), M128("Wb"), xcols(2 * h + j, aof(2 * h + j, t)), True, True) for j in range(2)])
        cp(ia(h, 0), ps(h, "S"))
        act(half("sold", 0, h), ps(h, "o1"), "Identity", float(2 ** 20))
        act(half("sold", 2, h), ps(h, "o2"), "Identity", float(2 ** 21))
        for j in range(2):
            cp(half("xa", 0, h, 32 * j, 32 * j + 32), xcols(2 * h + j, aof(2 * h + j, 0)), "AVG")
            cp(half("xo", 0, h, 32 * j, 32 * j + 32), xcols(2 * h + j, aof(2 * h + j, 1)), "AVG")
            cp(half("xo", 2, h, 32 * j, 32 * j + 32), xcols(2 * h + j, aof(2 * h + j, 2)), "AVG")

    def phase_a(t, h):
        tag[0] = "a%d%d" % (t, h)
        bx = (3 - t) * 2048; K = AB - bx; o = 1024 * h
        u = ia(h, 1); pi = ia(h, 5); st = half("st", t, h)
        hash_list(h, ia(h, 0), u, kcol, ia, "ku", LL(h, 0))
        ts(ia(h, 6), u, mcol, None, A.mult)
        ts(ia(h, 7), ia(h, 6), 4, 7, A.arith_shift_right, A.bitwise_and)
        cp(ps(h, "lf"), ia(h, 7))
        act(fa(h, 0), ps(h, "lf"), "Exp", 17 * LN2, 5 * LN2)
        tt(fa(h, 1), pi, ps(h, "lf"), A.add)
        ts(LL(h, 1), fa(h, 1), 3.0, None, A.add)
        tt(fa(h, 2), st, ps(h, "lf"), A.add)
        for j in range(2):
            ts(LL(h, 3, 32 * j, 32 * j + 32), fa(h, 2, 32 * j, 32 * j + 32), float(K + aof(2 * h + j, t) + 3), None, A.add)
        for lo, hi in chunks:
            cp(S("d1", o + lo, o + hi), IND("W", AB, AB + 4096, *gl(h, 0, lo, hi)), "AV")
        distance(h, "d1", half("xa", t, h), "r1", "D1")
        test(ps(h, "D1"), ps(h, "D1"), tcol, HUGE, A.is_lt, btcol, -HUGE)
        for lo, hi in chunks:
            cp(S("xe", o + lo, o + hi), IND("W", bx, AB, *gl(h, 3, lo, hi)), "AV")
            tt(S("d2", o + lo, o + hi), IND("W", AB, WEND, *gl(h, 1, lo, hi)), S("xe", o + lo, o + hi), A.subtract)
            act(S("r2", o + lo, o + hi), S("d2", o + lo, o + hi), "Abs")
        group(ps(h, "D2"), [(None, sel_m(m), S("r2", o + m, o + 1024, 16)) for m in range(16)])
        test(ps(h, "D2"), ps(h, "D2"), tcol, HUGE, A.is_lt, btcol, -HUGE)
        E = S("ba", 128 * h, 128 * h + 64)
        tt(fa(h, 3), ps(h, "D1"), fa(h, 0), A.min)
        tt(E, ps(h, "D2"), fa(h, 3), A.min)
        a0 = aof(2 * h, t)
        mm([(ps(h, "Q"), M128("BP"), E, True, True),
            (ps(h, "E"), M128("NI"), S("TH", 32 * a0, 32 * a0 + 64), True, False),
            (ps(h, "E"), M128("BO"), E, False, True)])
        test(ps(h, "Q"), ps(h, "Q"), 0.0, float(2 ** 17), A.is_lt, 0.0, -1.0)
        tt(fa(h, 4), ps(h, "Q"), pi, A.min)
        tt(fa(h, 5), ps(h, "E"), st, A.max)
        group(ps(h, "P"), [(None, M128("NI"), S("at", 32 * a0, 32 * a0 + 64)), (None, M128("BOf"), fa(h, 4))])
        tt(fa(h, 6), ps(h, "P"), fa(h, 5), A.min)
        ts(LL(h, 4), fa(h, 6), icol, float(K), A.add, A.add)
        tb = (2 - t) * 2048 + o
        for lo, hi in chunks:
            cp(S("W", tb + lo, tb + hi), IND("W", bx, WEND, *gl(h, 4, lo, hi)), "AV")
            add("scan", "V", (S("sc", o + lo, o + hi), S("msk", 0, hi - lo), S("W", tb + lo, tb + hi)),
                [S("sc", o + lo, o + hi)], [S("msk", 0, hi - lo), S("W", tb + lo, tb + hi)])

    def phase_b(t, h):
        tag[0] = "b%d%d" % (t, h)
        o = 1024 * h
        z = S("sc", o + 15, o + 1024, 16)
        mc = "mc%d" % t; pj = "pj%d" % t
        group(ps(h, "V"), [(None, S("Wj", 128 * t, 128 * t + 128), z)])
        if t < 2:
            cp(S("zc%d" % t, 64 * h, 64 * h + 64), z, "GAV")
        cp(ib(h, 0), ps(h, "V"))
        hash_list(h, ib(h, 0), half("vi", t, h), S(pj, 1, 2), ib, "kv", LL(h, 5))
        for lo, hi in chunks:
            cp(S("mg", o + lo, o + hi), IND(mc, 0, 4096, *gl(h, 5, lo, hi)), "AV")
        distance(h, "mg", z, "dm", "DM")
        ind = S("ba", 128 * h + 64, 128 * h + 128)
        test(ind, ps(h, "DM"), S(pj, 2, 3), 1.0, A.is_lt, S(pj, 2, 3), -1.0)
        known = (None, M128("BOB"), ind)

        def places(name, lhs, r):
            return [(ps(h, name, 32 * j, 32 * j + 32), lhs, tcols(t, 2 * h + j, aof(2 * h + j, r))) for j in range(2)]
        if t < 2:
            group(ps(h, "S"), [known] + places("S", M128("Wb"), t + 1))
            tt(ia(h, 0), ps(h, "S"), half("sold", t, h), A.min)
        group(ps(h, "L"), [(None, M128("ID"), S("s16", 64 * h, 64 * h + 64)), (None, M128("NI"), S("cst", 64 * t, 64 * t + 64)), known])
        tt(half("st", t + 1, h), ps(h, "L"), half("st", t, h), A.min)
        if t < 2:
            group(ps(h, "X"), [known] + places("X", M128("NI"), t + 1))
            tt(half("xy", 0, h), ps(h, "X"), half("xo", t, h), A.min)
            act(half("xa", t + 1, h), half("xy", 0, h), "Abs")
        if t == 0:
            group(ps(h, "S2"), [known, (None, M128("BO"), S("cst", 192, 256))] + places("S2", M128("Wb"), 2))
            tt(half("sold", 1, h), ps(h, "S2"), half("sold", 2, h), A.min)
            group(ps(h, "X2"), [known] + places("X2", M128("NI"), 2))
            tt(half("xy", 1, h), ps(h, "X2"), half("xo", 2, h), A.min)
            act(half("xo", 1, h), half("xy", 1, h), "Abs")

    def archive(t):
        tag[0] = "u%d" % t
        tt(fa(0, 7, 0, 32), ps(0, "L", 32 * t, 32 * t + 32), S("acon", 32 * t, 32 * t + 32), A.min)
        ts(LL(0, 6, 0, 32), fa(0, 7, 0, 32), icol, 2048.0 * (t + 2), A.add, A.add)
        cp(full("atmp"), IND("W", (2 - t) * 2048, WEND, "L", 64 * 6, 64 * 6 + 32), "AV")
        for i in range(16):
            cp(S("W", AB + 16 * t + i, AB + 2048, 64), S("atmp", i, 512, 16), "GAV")
        if t == 0:
            cp(S("W", AB + 4096, WEND), S("atmp", 0, 16), "GAV")

    def memory(t):
        tag[0] = "m%d" % t
        ts(M128("v32"), S("vi", 128 * t, 128 * t + 128), 31, None, A.bitwise_and)
        cp(M128("v32b"), M128("v32"))
        group(ps(1, "dg", 0, 8), [(None, M128("ID"), full("cd"))] + [(None, sel_m(r), S("v32b", r, 128, 16)) for r in range(16)])
        ts(full("mo%d" % t), ps(1, "dg", 0, 8), 8.0, c4r, A.mult, A.add)
        ks = (0, 1) if t == 0 else (2,)
        dist = (1, 2) if t == 0 else (1,)
        sz = send(full("zc%d" % t), [(d, full("zl%d" % k)) for d, k in zip(dist, ks)], "az%d" % t)
        sl = send(full("mo%d" % t), [(d, full("ml%d" % k)) for d, k in zip(dist, ks)], "az%d" % t)
        arrive("az%d" % t, list(dist) * 2, [full("zl%d" % k) for k in ks] + [full("ml%d" % k) for k in ks], [sz, sl])
        if t == 0:
            s2 = send(full("mown"), [(3, full("mc2"))], "am2"); s2["after"] = [sz["n"], sl["n"]]
            arrive("am2", [3], [full("mc2")], [s2])
        for k in ks:
            cp(IND("mc%d" % min(k + 1, 2), 0, 4096, "ml%d" % k, 0, 8), full("zl%d" % k))

    for t in range(3):
        phase_a(t, 0); phase_a(t, 1); phase_b(t, 0)
        if t < 2:
            archive(t)
        phase_b(t, 1)
        if t < 2:
            memory(t)
    tag[0] = "y"
    for cls in range(4):
        ts(S("Ly", cls, 128, 4), S("st", 384 + 32 * cls, 384 + 32 * cls + 32), icol, float(AB), A.add, A.add)
    w = cfg["yg"]
    for x in range(0, 2048, w):
        cp(S("yb", x, x + w), IND("W", 0, AB, "Ly", x // 16, (x + w) // 16), "AV")
    for j, (lo, hi) in enumerate(zip(cfg["ys"], cfg["ys"][1:])):
        add("dma", "S", (S("yb", lo, hi), "y", lo, hi, False), [], [S("yb", lo, hi)], sem="sy%d" % j, nb=256 * (hi - lo))
    return ops


def hazards(ops):
    hist = {}
    deps = []
    for j, op in enumerate(ops):
        d = set()
        for b, m in op["r"]:
            d.update(i for i, mi, isw in hist.get(b, []) if isw and mi & m)
        for b, m in op["w"]:
            d.update(i for i, mi, isw in hist.get(b, []) if mi & m)
        for b, m in op["w"]:
            hist[b] = [(i, mi & ~m, isw) for i, mi, isw in hist.get(b, []) if mi & ~m] + [(j, m, True)]
        for b, m in op["r"]:
            hist.setdefault(b, []).append((j, m, False))
        deps.append(sorted(d))
    return deps


def make_plan(cfg, order, queues):
    ops = build_ops(cfg)
    deps = hazards(ops)
    pos = {j: x for x, j in enumerate(order)}
    assert sorted(order) == list(range(len(ops)))
    tick = {}
    cnt = {e: 0 for e in "VAPG"}
    know = {e: {} for e in "VAPGS"}
    seen = {}
    steps = []
    bank_last = {}
    for j in order:
        op = ops[j]; e = queues[j]
        assert e in op["engs"] and all(pos[i] < pos[j] for i in deps[j] + op["after"])
        if e == "N":
            tick[j] = (op["sem"], 1); seen[j] = {op["sem"]: 1}
            continue
        need = list(deps[j])
        for b in sorted(set(b for b, m in op["r"] + op["w"] if SCRATCH[b][0] == "psum")):
            need += [i for e2, i in bank_last.get(b, {}).items() if e2 != e]
            bank_last.setdefault(b, {})[e] = j
        need = [i for i in need if ops[i]["k"] != "rem" and not (e == "P" and queues[i] == "P")]
        best = {}
        for i in need:
            s, v = tick[i]
            if v > best.get(s, (0, 0))[0]:
                best[s] = (v, i)
        waits = []
        kn = know[e]
        for s, (v, i) in sorted(best.items(), key=lambda x: -pos[x[1][1]]):
            if kn.get(s, 0) >= v:
                continue
            waits.append((s, v))
            for s2, v2 in seen[i].items():
                if kn.get(s2, 0) < v2:
                    kn[s2] = v2
        if op["k"] == "dma":
            tick[j] = (op["sem"], 1)
        elif op["k"] != "rem":
            cnt[e] += 1; tick[j] = ("c" + e, cnt[e])
        if j in tick:
            seen[j] = dict(kn); seen[j][tick[j][0]] = tick[j][1]
        steps.append((op, e, waits))
    return {"steps": steps, "cnt": cnt, "ops": ops}


PLAN = {}


def rank_program(g, core, T, topo):
    rank = T.rank_of(core)
    if rank is None:
        return
    if "p" not in PLAN:
        PLAN["p"] = make_plan(CFG, [int(x) for x in ORDER.split()], QUEUES)
    plan = PLAN["p"]
    queue = {"V": g.vector, "A": g.scalar, "P": g.tensor, "G": g, "S": g.sync}
    F = {"Exp": ActivationFunctionType.Exp, "Abs": ActivationFunctionType.Abs, "Relu": ActivationFunctionType.Relu,
         "Identity": ActivationFunctionType.Identity}
    total = {}
    for op in plan["ops"]:
        if op["k"] == "arr":
            total[op["sem"]] = sum(len(topo.engines(T.cores[(rank + d) % N], core)) for d in op["a"][0])
        elif op["k"] == "dma":
            total[op["sem"]] = 16

    def ap(o):
        if not isinstance(o, tuple):
            return o
        if o[0] == "i":
            return T[o[1]][:, o[2]:o[3]].indirect(T[o[4]][:, o[5]:o[6]])
        if o[4] == 1:
            return T[o[1]][:, o[2]:o[3]]
        return T[o[1]][:, o[2]:o[3]:o[4]]

    sent = 0
    for op, e, waits in plan["steps"]:
        q = queue[e]; k = op["k"]; a = op["a"]
        if e == "A" and "alt" in op:
            k = "act"; a = op["alt"]
        for s, v in waits:
            q.wait_ge(T.sem[s], total.get(s, v))
        if k == "dma":
            hbm = T[a[1]][:, a[2]:a[3]]
            (q.dma_start(ap(a[0]), hbm) if a[4] else q.dma_start(hbm, ap(a[0]))).then_inc(T.sem[op["sem"]], 16)
            continue
        if k == "rem":
            cores = [T.cores[(rank - d) % N] for d, o in a[1]]
            mask = topo.mask(core, cores[0])
            if len(cores) == 1:
                rid, pid, se = topo.addr(cores[0])
                g.remote_dma(ap(a[1][0][1]), ap(a[0]), T.sem[a[2]], T.sem.sent, pid, rid, mask)
            else:
                ids = [DstId(rid=topo.addr(c)[0], pnc=topo.addr(c)[1]) for c in cores]
                g.remote_dma_fused([RemoteDMATransfer(dst_ids=ids, dma_engine_mask=mask, remote_sem=T.sem[a[2]],
                                                      srcs=[ap(a[0])], dsts=[ap(o) for d, o in a[1]])], local_sem=T.sem.sent)
            sent += len(topo.engines(core, cores[0]))
            continue
        if k == "mm":
            for o, l, r, st, sp in a:
                ins = q.matmul(ap(o), ap(l), ap(r), st, sp)
        elif k == "tt":
            ins = q.tensor_tensor(ap(a[0]), ap(a[1]), ap(a[2]), a[3])
        elif k == "ts":
            if a[5] is None:
                ins = q.tensor_scalar(ap(a[0]), ap(a[1]), ap(a[2]), None, a[4])
            else:
                ins = q.tensor_scalar(ap(a[0]), ap(a[1]), ap(a[2]), ap(a[3]), a[4], a[5])
        elif k == "cp":
            if e == "A":
                ins = q.activation(ap(a[0]), ap(a[1]), ActivationFunctionType.Copy)
            elif e == "G":
                ins = g.affine_select(ap(a[0]), ap(a[1]), [[0, count(a[0])]], AluOpType.is_gt, 0.0, 1, 0)
            else:
                ins = q.tensor_copy(ap(a[0]), ap(a[1]))
        elif k == "ms":
            ins = q.memset(ap(a[0]), a[1])
        elif k == "act":
            ins = q.activation(ap(a[0]), ap(a[1]), F[a[2]], bias=ap(a[3]), scale=ap(a[4]))
        elif k == "scan":
            ins = q.tensor_tensor_scan(ap(a[0]), ap(a[1]), ap(a[2]), 0.0, AluOpType.mult, AluOpType.max)
        elif k == "iota":
            if SCRATCH[a[0][1]][2] == "int32":
                ins = g.iota(ap(a[0]), a[1], a[2], a[3])
            else:
                ins = g.iota(ap(a[0]), a[1], a[2], a[3], allow_small_or_imprecise_dtypes=True)
        else:
            ins = g.affine_select(ap(a[0]), ap(a[1]), a[2], a[3], a[4], a[5], a[6])
        ins.then_inc(T.sem["c" + e], 1)
    for e in "VAPG":
        g.wait_ge(T.sem["c" + e], plan["cnt"][e])
    g.wait_ge(T.sem.sent, sent)
    for s in sorted(total):
        g.wait_ge(T.sem[s], total[s])
